import numpy as np
import ml_dtypes


def mxq(x, axis, fmt="e4m3"):
    dtype, down = {"e4m3": (ml_dtypes.float8_e4m3fn, 7), "e5m2": (ml_dtypes.float8_e5m2, 14)}[fmt]
    v = np.moveaxis(np.asarray(x, np.float32).astype(ml_dtypes.bfloat16).astype(np.float64), axis, -1)
    blocks = v.reshape(v.shape[:-1] + (-1, 32))
    amax = np.abs(blocks).max(-1, keepdims=True)
    byte = np.maximum(np.where(amax > 0, np.frexp(amax)[1] - 1 + 127, 0) - down, 1)
    scale = np.exp2(byte - 127.0)
    codes = (blocks / scale).astype(np.float32).astype(dtype).astype(np.float64)
    return np.moveaxis((codes * scale).reshape(v.shape), -1, axis)


WIDE = False


def mx_kscale(k):
    if not WIDE:
        return np.ones(k)
    levels = np.array([24, -24, 12, -12, 0])
    if k % 512:
        return np.exp2(np.random.permutation(np.resize(levels, k // 32))).repeat(32)
    a = np.empty((k // 512, 16))
    for p in range(k // 512):
        a[p, :8] = np.random.permutation(np.resize(levels, 8))
        for g in range(8):
            far = levels[np.abs(levels - a[p, g]) >= 10]
            a[p, g + 8] = far[np.random.randint(len(far))]
    return np.exp2(a.ravel()).repeat(32)


def f64(x):
    return np.asarray(x).astype(np.float64)


def striped(idx):
    return np.tile(idx.reshape(-1, 16).T, (8, 1)).astype(np.uint16)


def unstriped(offs):
    return offs[:16].T.reshape(-1).astype(np.int64)


def striped8(idx):
    return np.concatenate([v.reshape(-1, 16).T for v in idx]).astype(np.uint16)


def unstriped8(offs):
    return np.stack([offs[16 * g:16 * g + 16].T.reshape(-1) for g in range(8)]).astype(np.int64)


E2M1 = np.array([0.0, 0.5, 1.0, 1.5, 2.0, 3.0, 4.0, 6.0, -0.0, -0.5, -1.0, -1.5, -2.0, -3.0, -4.0, -6.0])


def pack_weight(w, fmt):
    k, n = w.shape
    w = f64(np.asarray(w, np.float32).astype(ml_dtypes.bfloat16)).reshape(k // 32, 32, n)
    amax = np.abs(w).max(1)
    if fmt == "e4m3":
        byte = np.frexp(amax)[1] - 1 + 127 - 7
    else:
        mant, ex = np.frexp(amax / 6.0)
        byte = np.where(mant > 0.5, ex, ex - 1) + 127
    byte = np.clip(np.where(amax > 0, byte, 1), 1, 254)
    scaled = (w * np.exp2(127.0 - byte)[:, None, :]).reshape(k, n).astype(np.float32)
    by_word = np.ascontiguousarray(scaled.reshape(k // 512, 128, 4, n).transpose(0, 1, 3, 2))
    if fmt == "e4m3":
        words = by_word.astype(ml_dtypes.float8_e4m3fn).view(np.uint8)
    else:
        c = by_word.astype(ml_dtypes.float4_e2m1fn).view(np.uint8) & 0xF
        words = (c[..., 0::2] | (c[..., 1::2] << 4)).reshape(k // 512, 128, 2 * n)
    return np.ascontiguousarray(words), np.ascontiguousarray(byte.astype(np.uint8).reshape(k // 512, 16, n))


def unpack_weight(words, scales, fmt):
    g, _, n = scales.shape
    words = np.ascontiguousarray(words).reshape(g, 128, n, -1)
    if fmt == "e4m3":
        vals = words.view(ml_dtypes.float8_e4m3fn).astype(np.float64)
    else:
        nib = np.empty((g, 128, n, 4), np.uint8)
        nib[..., 0::2] = words & 0xF
        nib[..., 1::2] = words >> 4
        vals = E2M1[nib]
    vals = vals * np.repeat(np.exp2(scales.astype(np.float64) - 127.0), 8, axis=1)[..., None]
    return vals.transpose(0, 1, 3, 2).reshape(g * 512, n)


def pack_table4(v):
    words, scales = pack_weight(v, "e2m1")
    g, t = words.shape[0] // 2, v.shape[1]
    return np.ascontiguousarray(words.reshape(g, 2, 128, t, 2).transpose(0, 2, 3, 1, 4).reshape(g, 128, t, 4)), scales


def unpack_table4(words, scales):
    g, _, t, _ = words.shape
    return unpack_weight(words.reshape(g, 128, t, 2, 2).transpose(0, 3, 1, 2, 4).reshape(2 * g, 128, 2 * t), scales, "e2m1")


def planes(y):
    n, m = y.shape
    v = y.astype(np.float32).astype(ml_dtypes.bfloat16).astype(np.float64).reshape(n // 32, 32, m)
    top = np.abs(v).max(1)
    byte = np.clip(np.where(top > 0, np.frexp(top)[1] - 1 + 127 - 7, 1), 1, 254)
    codes = (v * np.exp2(127.0 - byte)[:, None, :]).reshape(n, m).astype(np.float32).astype(ml_dtypes.float8_e4m3fn).view(np.uint8)
    words = codes.reshape(n // 512, 128, 4, m).transpose(0, 1, 3, 2)
    return np.ascontiguousarray(words), np.ascontiguousarray(byte.astype(np.uint8).reshape(n // 512, 16, m))


def sigm(f):
    return 1.0 / (1.0 + np.exp(-np.maximum(f, -700.0)))


K, L, R, N, T, J = 512, 1024, 512, 512, 2048, 1024


def setup_inputs():
    n = np.random.standard_normal
    s = mx_kscale(K)[:, None]
    s2 = mx_kscale(L)[:, None]
    u = mx_kscale(R)[:, None]
    p_tab = pack_table4(n((L, T)) * s2)
    p_wb = pack_weight(n((L, R)) / np.sqrt(L) / s2, "e2m1")
    p_wd = pack_weight(n((R, N)) / np.sqrt(R) / u, "e4m3")
    return {
        "tab_words": p_tab[0],
        "tab_scales": p_tab[1],
        "xT": (n((K, T)) * s).astype(np.float32),
        "wgt2": np.repeat(np.random.uniform(0.5, 2.0, (8, J)), 16, axis=0).astype(np.float32),
        "wa": (n((K, R)) / np.sqrt(K) / s * u.T).astype(np.float32),
        "wb_words": p_wb[0],
        "wb_scales": p_wb[1],
        "wd_words": p_wd[0],
        "wd_scales": p_wd[1],
        "offs": striped(np.random.permutation(T)[:J]),
        "offs2": striped8(np.stack([np.random.permutation(T)[:J] for _ in range(8)])),
    }


def reference(tab_words, tab_scales, xT, wgt2, wa, wb_words, wb_scales, wd_words, wd_scales, offs, offs2):
    idx = unstriped(offs)
    idx2 = unstriped8(offs2)
    tab_ = unpack_table4(tab_words, tab_scales)[:, idx]
    rows = np.arange(K)
    xg = f64(wgt2)[rows // 4 % 128] * f64(xT)[rows[:, None], idx2[rows % 512 // 64]]
    xT_ = mxq(xg, 0, "e4m3")
    wa_ = mxq(f64(wa), 0, "e4m3")
    wb_ = unpack_weight(wb_words, wb_scales, "e2m1")
    ya = wa_.T @ xT_
    yb = wb_.T @ tab_
    h = ya * sigm(yb)
    h_ = mxq(h, 0, "e4m3")
    wd_ = unpack_weight(wd_words, wd_scales, "e4m3")
    y = wd_.T @ h_
    return (y,) + planes(y)

@@ -1,0 +1,246 @@
+from contextlib import ExitStack
+
+import concourse.mybir as mybir
+
+K, L, R, N, T, J = 512, 1024, 512, 512, 2048, 1024
+FLOPS = 2 * J * (K * R + L * R + R * N)
+
+F32 = mybir.dt.float32
+BF16 = mybir.dt.bfloat16
+I32 = mybir.dt.int32
+U32 = mybir.dt.uint32
+U16 = mybir.dt.uint16
+U8 = mybir.dt.uint8
+FP8X4 = mybir.dt.float8_e4m3fn_x4
+FP4X4 = mybir.dt.float4_e2m1fn_x4
+MULT = mybir.AluOpType.mult
+SIGMOID = mybir.ActivationFunctionType.Sigmoid
+
+P = 128
+PACK = 4
+CH = 128
+NCH = J // CH
+GW = 256
+NG = J // GW
+
+
+def tile_list_htabg_gate_noneP_kernel(
+    tc, tab_words, tab_scales, xT, wgt2, wa, wb_words, wb_scales, wd_words, wd_scales, offs, offs2, out_0, out_1, out_2
+):
+    nc = tc.nc
+    with ExitStack() as ctx:
+        keep = ctx.enter_context(tc.tile_pool(name="keep", bufs=1))
+        ring = ctx.enter_context(tc.tile_pool(name="ring", bufs=3))
+        psum = ctx.enter_context(tc.psum_pool(name="psum", bufs=1))
+
+        idx = keep.tile([P, J // 16], U16, name="idx")
+        idx2 = keep.tile([P, J // 16], U16, name="idx2")
+        tsc = keep.tile([P, T], U8, name="tsc", align_bytes=64)
+        wsc = keep.tile([P, 2, R], U8, name="wsc", align_bytes=64)
+        tabw = keep.tile([P, T], I32, name="tabw", align_bytes=64)
+        wb_raw = keep.tile([P, 2, R // 2], I32, name="wb_raw", align_bytes=64)
+        wd_raw = keep.tile([P, N], I32, name="wd_raw", align_bytes=64)
+        wgt = keep.tile([P, J], F32, name="wgt", align_bytes=64)
+        wa_raw = keep.tile([P, PACK, R], F32, name="wa_raw", align_bytes=64)
+        xp = [keep.tile([P, T], F32, name="xp%d" % i, align_bytes=64) for i in range(PACK)]
+        tsc1 = keep.tile([P, J], U8, name="tsc1", align_bytes=64)
+        dsc = keep.tile([P, N], U8, name="dsc", align_bytes=64)
+
+        nc.gpsimd.memset(tsc[:].bitcast(I32), 0)
+        nc.gpsimd.memset(wsc[:].bitcast(I32), 0)
+        nc.vector.memset(tsc1[:].bitcast(I32), 0)
+        nc.vector.memset(dsc[:].bitcast(I32), 0)
+        nc.sync.dma_start(idx[:], offs)
+        nc.sync.dma_start(wb_raw[:], wb_words.rearrange("a p n -> p a n").bitcast(I32))
+        for q in range(4):
+            nc.sync.dma_start(tsc[32 * q : 32 * q + 8, :].bitcast(I32), tab_scales[:, 4 * q : 4 * q + 4, :].bitcast(I32))
+        nc.sync.dma_start(tabw[:], tab_words[0].rearrange("p t b -> p (t b)").bitcast(I32))
+        nc.sync.dma_start(idx2[:], offs2)
+        for q in range(4):
+            nc.gpsimd.dma_start(
+                wsc[32 * q : 32 * q + 4, :, :].bitcast(I32),
+                wb_scales[:, 4 * q : 4 * q + 4, :].rearrange("a r n -> r a n").bitcast(I32),
+            )
+        for q in range(4):
+            nc.gpsimd.dma_start(dsc[32 * q : 32 * q + 4, :].bitcast(I32), wd_scales[0, 4 * q : 4 * q + 4, :].bitcast(I32))
+        x_planes = xT.rearrange("(p i) t -> i p t", i=PACK)
+        nc.sync.dma_start(wgt[:], wgt2)
+        nc.sync.dma_start(xp[0][:], x_planes[0])
+        nc.sync.dma_start(xp[1][:], x_planes[1])
+        nc.sync.dma_start(xp[2][:], x_planes[2])
+        nc.sync.dma_start(wa_raw[:], wa.rearrange("(p i) r -> p i r", i=PACK))
+        nc.sync.dma_start(xp[3][:], x_planes[3])
+        nc.sync.dma_start(wd_raw[:], wd_words[0].rearrange("p n b -> p (n b)").bitcast(I32))
+
+        wbp = keep.tile([P, 2, 2 * R], U8, name="wbp", align_bytes=64)
+        nc.vector.tensor_copy(
+            wbp[:].bitcast(U16).rearrange("p a (t c i) -> p a c t i", t=PACK, i=8),
+            wb_raw[:].bitcast(U16).rearrange("p a (c i t) -> p a c t i", t=PACK, i=8),
+        )
+        tsc0 = keep.tile([P, J], U8, name="tsc0", align_bytes=64)
+        nc.vector.tensor_copy(tsc0[:], tsc[:].indirect(idx[:]))
+        nc.sync.dma_start(tsc1[0 : P - 4, :].bitcast(I32), tsc0[4:P, :].bitcast(I32))
+        gw = keep.tile([P, J], U32, name="gw", align_bytes=64)
+        nc.vector.tensor_copy(gw[:], tabw[:].bitcast(U32).indirect(idx[:]))
+        tw = keep.tile([P, 2, 2 * J], U8, name="tw", align_bytes=64)
+        nc.vector.tensor_copy(tw[:].bitcast(U16), gw[:].bitcast(U16).rearrange("p (j d) -> p d j", d=2))
+
+        wscp = keep.tile([P, 2, R], U8, name="wscp", align_bytes=64)
+        dscp = keep.tile([P, N], U8, name="dscp", align_bytes=64)
+        nc.vector.tensor_copy(
+            wscp[:].rearrange("p a (t c i) -> p a c t i", t=PACK, i=16),
+            wsc[:].rearrange("p a (c i t) -> p a c t i", t=PACK, i=16),
+        )
+
+        tscs = (tsc0, tsc1)
+        sig = []
+        for c in range(NCH):
+            yb = psum.tile([P, PACK, CH], F32, name="yb", tag="yb", bufs=2)
+            for t in range(PACK):
+                for a in range(2):
+                    nc.tensor.matmul_mx(
+                        out=yb[:, t, :],
+                        lhsT=wbp[:, a, 2 * P * t : 2 * P * (t + 1)].bitcast(FP4X4),
+                        lhsT_scale=wscp[:, a, P * t : P * (t + 1)],
+                        rhs=tw[:, a, 2 * CH * c : 2 * CH * (c + 1)].bitcast(FP4X4),
+                        rhs_scale=tscs[a][:, CH * c : CH * (c + 1)],
+                        start=(a == 0),
+                        stop=(a == 1),
+                    )
+            s = keep.tile([P, CH, PACK], F32, name="sig%d" % c, align_bytes=64)
+            nc.scalar.activation(s[:], yb[:].rearrange("p t n -> p n t"), SIGMOID)
+            sig.append(s)
+
+        xg = [keep.tile([P, PACK, GW], F32, name="xg%d" % g, align_bytes=64) for g in range(NG)]
+
+        def gather(i, g):
+            nc.vector.tensor_tensor(
+                xg[g][:, i, :], xp[i][:].indirect(idx2[:, g * GW // 16 : (g + 1) * GW // 16]), wgt[:, g * GW : (g + 1) * GW], MULT
+            )
+
+        for i in range(PACK - 1):
+            for g in range(NG):
+                gather(i, g)
+
+        nc.vector.tensor_copy(
+            dscp[:].rearrange("p (t c i) -> p c t i", t=PACK, i=16), dsc[:].rearrange("p (c i t) -> p c t i", t=PACK, i=16)
+        )
+        wa_bf = keep.tile([P, R * PACK], BF16, name="wa_bf", align_bytes=64)
+        nc.scalar.copy(
+            wa_bf[:].rearrange("p (t m i) -> p m i t", t=PACK, i=PACK), wa_raw[:].rearrange("p i (m t) -> p m i t", t=PACK)
+        )
+        wa_q = keep.tile([P, R], U32, name="wa_q", align_bytes=64)
+        wa_s = keep.tile([P, R], U8, name="wa_s", align_bytes=64)
+        wdp = keep.tile([P, N], I32, name="wdp", align_bytes=64)
+
+        x_q = keep.tile([P, J], U32, name="x_q", align_bytes=64)
+        x_s = keep.tile([P, J], U8, name="x_s", align_bytes=64)
+        h_q = keep.tile([P, J], U32, name="h_q", align_bytes=64)
+        h_s = keep.tile([P, J], U8, name="h_s", align_bytes=64)
+        y_q = keep.tile([P, J], U32, name="y_q", align_bytes=64)
+        y_s = keep.tile([P, J], U8, name="y_s", align_bytes=64)
+        out_rows = out_0.rearrange("(p t) j -> p t j", t=PACK)
+        out_words = out_1[0].rearrange("p j b -> p (j b)").bitcast(I32)
+
+        x_bf = {}
+        ya = {}
+        h_bf = {}
+        yp = {}
+        y_bf = {}
+
+        def round_x(g):
+            x_bf[g] = ring.tile([P, GW * PACK], BF16, name="x_bf", align_bytes=64)
+            nc.scalar.copy(
+                x_bf[g][:].rearrange("p (c e i) -> p c i e", i=PACK, e=4), xg[g][:].rearrange("p i (c e) -> p c i e", e=4)
+            )
+
+        def quant_x(g):
+            cols = slice(g * GW, (g + 1) * GW)
+            nc.vector.quantize_mx(out=x_q[:, cols].bitcast(FP8X4), scales=x_s[:, cols], in_=x_bf[g][:])
+
+        def mm_a(c):
+            cols = slice(c * CH, (c + 1) * CH)
+            ya[c] = psum.tile([P, PACK, CH], F32, name="ya", tag="ya", bufs=3)
+            for t in range(PACK):
+                nc.tensor.matmul_mx(
+                    out=ya[c][:, t, :],
+                    lhsT=wa_q[:, P * t : P * (t + 1)].bitcast(FP8X4),
+                    lhsT_scale=wa_s[:, P * t : P * (t + 1)],
+                    rhs=x_q[:, cols].bitcast(FP8X4),
+                    rhs_scale=x_s[:, cols],
+                    start=True,
+                    stop=True,
+                )
+
+        def gate(c):
+            h_bf[c] = ring.tile([P, CH, PACK], BF16, name="h_bf", align_bytes=64)
+            nc.vector.tensor_tensor(h_bf[c][:], ya[c][:].rearrange("p t n -> p n t"), sig[c][:], MULT)
+
+        def quant_h(c):
+            cols = slice(c * CH, (c + 1) * CH)
+            nc.vector.quantize_mx(
+                out=h_q[:, cols].bitcast(FP8X4), scales=h_s[:, cols], in_=h_bf[c][:].rearrange("p n t -> p (n t)")
+            )
+
+        def mm_d(c):
+            cols = slice(c * CH, (c + 1) * CH)
+            yp[c] = psum.tile([P, PACK, CH], F32, name="yp", tag="yp", bufs=3)
+            for t in range(PACK):
+                nc.tensor.matmul_mx(
+                    out=yp[c][:, t, :],
+                    lhsT=wdp[:, P * t : P * (t + 1)].bitcast(FP8X4),
+                    lhsT_scale=dscp[:, P * t : P * (t + 1)],
+                    rhs=h_q[:, cols].bitcast(FP8X4),
+                    rhs_scale=h_s[:, cols],
+                    start=True,
+                    stop=True,
+                )
+
+        def out_y(c):
+            cols = slice(c * CH, (c + 1) * CH)
+            y_sb = ring.tile([P, PACK, CH], F32, name="y_sb", align_bytes=64, bufs=4)
+            y_bf[c] = ring.tile([P, CH * PACK], BF16, name="y_bf", align_bytes=64)
+            nc.scalar.copy(y_sb[:], yp[c][:])
+            if c % 2 == 0:
+                nc.scalar.copy(y_bf[c][:].rearrange("p (n t) -> p n t", t=PACK), yp[c][:].rearrange("p t n -> p n t"))
+            else:
+                nc.vector.tensor_copy(
+                    y_bf[c][:].rearrange("p (c e t) -> p c t e", t=PACK, e=4), y_sb[:].rearrange("p t (c e) -> p c t e", e=4)
+                )
+            nc.sync.dma_start(out_rows[:, :, cols], y_sb[:])
+
+        def quant_y(c):
+            cols = slice(c * CH, (c + 1) * CH)
+            nc.vector.quantize_mx(out=y_q[:, cols].bitcast(FP8X4), scales=y_s[:, cols], in_=y_bf[c][:])
+            if c % 2 == 1:
+                pair = slice((c - 1) * CH, (c + 1) * CH)
+                nc.sync.dma_start(out_words[:, pair], y_q[:, pair].bitcast(I32))
+
+        gather(PACK - 1, 0)
+        round_x(0)
+        nc.vector.quantize_mx(out=wa_q[:].bitcast(FP8X4), scales=wa_s[:], in_=wa_bf[:])
+        gather(PACK - 1, 1)
+        round_x(1)
+        quant_x(0)
+        nc.vector.tensor_copy(
+            wdp[:].rearrange("p (t c i) -> p c t i", t=PACK, i=4), wd_raw[:].rearrange("p (c i t) -> p c t i", t=PACK, i=4)
+        )
+        for step in range(NCH + 3):
+            if step % 2 == 0 and step // 2 + 2 < NG:
+                gather(PACK - 1, step // 2 + 2)
+                round_x(step // 2 + 2)
+            if step % 2 == 1 and (step + 1) // 2 < NG:
+                quant_x((step + 1) // 2)
+            if step < NCH:
+                mm_a(step)
+                gate(step)
+            if 0 <= step - 1 < NCH:
+                quant_h(step - 1)
+                mm_d(step - 1)
+            if 0 <= step - 2 < NCH:
+                out_y(step - 2)
+            if 0 <= step - 3 < NCH:
+                quant_y(step - 3)
+        for q in range(4):
+            eng = nc.scalar if q % 2 else nc.sync
+            eng.dma_start(out_2[0, 4 * q : 4 * q + 4, :].bitcast(I32), y_s[32 * q : 32 * q + 4, :].bitcast(I32))

@@ -43,26 +43,27 @@ def tile_list_htabg_gate_noneP_kernel(
         wgt = keep.tile([P, J], F32, name="wgt", align_bytes=64)
         wa_raw = keep.tile([P, PACK, R], F32, name="wa_raw", align_bytes=64)
         xp = [keep.tile([P, T], F32, name="xp%d" % i, align_bytes=64) for i in range(PACK)]
+        tsc0 = keep.tile([P, J], U8, name="tsc0", align_bytes=64)
         tsc1 = keep.tile([P, J], U8, name="tsc1", align_bytes=64)
         dsc = keep.tile([P, N], U8, name="dsc", align_bytes=64)
 
-        nc.gpsimd.memset(tsc[:].bitcast(I32), 0)
         nc.gpsimd.memset(wsc[:].bitcast(I32), 0)
-        nc.vector.memset(tsc1[:].bitcast(I32), 0)
-        nc.vector.memset(dsc[:].bitcast(I32), 0)
-        nc.sync.dma_start(idx[:], offs)
-        nc.sync.dma_start(wb_raw[:], wb_words.rearrange("a p n -> p a n").bitcast(I32))
         for q in range(4):
-            nc.sync.dma_start(tsc[32 * q : 32 * q + 8, :].bitcast(I32), tab_scales[:, 4 * q : 4 * q + 4, :].bitcast(I32))
+            nc.vector.memset(tsc[32 * q : 32 * q + 24, :].bitcast(I32), 0)
+        nc.gpsimd.memset(tsc0[:].bitcast(I32), 0)
+        nc.gpsimd.memset(tsc1[:].bitcast(I32), 0)
+        nc.gpsimd.memset(dsc[:].bitcast(I32), 0)
+        nc.sync.dma_start(idx[:], offs)
+        for q in range(4):
+            nc.sync.dma_start(tsc[32 * q + 24 : 32 * q + 32, :].bitcast(I32), tab_scales[:, 4 * q : 4 * q + 4, :].bitcast(I32))
+        nc.sync.dma_start(wb_raw[:], wb_words.rearrange("a p n -> p a n").bitcast(I32))
         nc.sync.dma_start(tabw[:], tab_words[0].rearrange("p t b -> p (t b)").bitcast(I32))
         nc.sync.dma_start(idx2[:], offs2)
         for q in range(4):
-            nc.gpsimd.dma_start(
+            nc.sync.dma_start(
                 wsc[32 * q : 32 * q + 4, :, :].bitcast(I32),
                 wb_scales[:, 4 * q : 4 * q + 4, :].rearrange("a r n -> r a n").bitcast(I32),
             )
-        for q in range(4):
-            nc.gpsimd.dma_start(dsc[32 * q : 32 * q + 4, :].bitcast(I32), wd_scales[0, 4 * q : 4 * q + 4, :].bitcast(I32))
         x_planes = xT.rearrange("(p i) t -> i p t", i=PACK)
         nc.sync.dma_start(wgt[:], wgt2)
         nc.sync.dma_start(xp[0][:], x_planes[0])
@@ -72,21 +73,23 @@ def tile_list_htabg_gate_noneP_kernel(
         nc.sync.dma_start(xp[3][:], x_planes[3])
         nc.sync.dma_start(wd_raw[:], wd_words[0].rearrange("p n b -> p (n b)").bitcast(I32))
 
+        for q in range(4):
+            nc.sync.dma_start(dsc[32 * q : 32 * q + 4, :].bitcast(I32), wd_scales[0, 4 * q : 4 * q + 4, :].bitcast(I32))
+        tscg = keep.tile([P, J], U8, name="tscg", align_bytes=64)
+        nc.vector.tensor_copy(tscg[:], tsc[:].indirect(idx[:]))
+        nc.scalar.dma_start(tsc0[0 : P - 28, :].bitcast(I32), tscg[24 : P - 4, :].bitcast(I32))
+        nc.scalar.dma_start(tsc1[0 : P - 28, :].bitcast(I32), tscg[28:P, :].bitcast(I32))
         wbp = keep.tile([P, 2, 2 * R], U8, name="wbp", align_bytes=64)
         nc.vector.tensor_copy(
             wbp[:].bitcast(U16).rearrange("p a (t c i) -> p a c t i", t=PACK, i=8),
             wb_raw[:].bitcast(U16).rearrange("p a (c i t) -> p a c t i", t=PACK, i=8),
         )
-        tsc0 = keep.tile([P, J], U8, name="tsc0", align_bytes=64)
-        nc.vector.tensor_copy(tsc0[:], tsc[:].indirect(idx[:]))
-        nc.sync.dma_start(tsc1[0 : P - 4, :].bitcast(I32), tsc0[4:P, :].bitcast(I32))
         gw = keep.tile([P, J], U32, name="gw", align_bytes=64)
         nc.vector.tensor_copy(gw[:], tabw[:].bitcast(U32).indirect(idx[:]))
         tw = keep.tile([P, 2, 2 * J], U8, name="tw", align_bytes=64)
         nc.vector.tensor_copy(tw[:].bitcast(U16), gw[:].bitcast(U16).rearrange("p (j d) -> p d j", d=2))
 
         wscp = keep.tile([P, 2, R], U8, name="wscp", align_bytes=64)
-        dscp = keep.tile([P, N], U8, name="dscp", align_bytes=64)
         nc.vector.tensor_copy(
             wscp[:].rearrange("p a (t c i) -> p a c t i", t=PACK, i=16),
             wsc[:].rearrange("p a (c i t) -> p a c t i", t=PACK, i=16),
@@ -122,16 +125,13 @@ def tile_list_htabg_gate_noneP_kernel(
             for g in range(NG):
                 gather(i, g)
 
-        nc.vector.tensor_copy(
-            dscp[:].rearrange("p (t c i) -> p c t i", t=PACK, i=16), dsc[:].rearrange("p (c i t) -> p c t i", t=PACK, i=16)
-        )
-        wa_bf = keep.tile([P, R * PACK], BF16, name="wa_bf", align_bytes=64)
+        wa_bf = keep.tile([P, R * PACK], BF16, name="wa_bf", tag="tw", align_bytes=64)
         nc.scalar.copy(
             wa_bf[:].rearrange("p (t m i) -> p m i t", t=PACK, i=PACK), wa_raw[:].rearrange("p i (m t) -> p m i t", t=PACK)
         )
         wa_q = keep.tile([P, R], U32, name="wa_q", align_bytes=64)
         wa_s = keep.tile([P, R], U8, name="wa_s", align_bytes=64)
-        wdp = keep.tile([P, N], I32, name="wdp", align_bytes=64)
+        wdp = keep.tile([P, N], I32, name="wdp", tag="xp2", align_bytes=64)
 
         x_q = keep.tile([P, J], U32, name="x_q", align_bytes=64)
         x_s = keep.tile([P, J], U8, name="x_s", align_bytes=64)
@@ -224,6 +224,10 @@ def tile_list_htabg_gate_noneP_kernel(
         quant_x(0)
         nc.vector.tensor_copy(
             wdp[:].rearrange("p (t c i) -> p c t i", t=PACK, i=4), wd_raw[:].rearrange("p (c i t) -> p c t i", t=PACK, i=4)
+        )
+        dscp = keep.tile([P, N], U8, name="dscp", tag="wa_raw", align_bytes=64)
+        nc.vector.tensor_copy(
+            dscp[:].rearrange("p (t c i) -> p c t i", t=PACK, i=16), dsc[:].rearrange("p (c i t) -> p c t i", t=PACK, i=16)
         )
         for step in range(NCH + 3):
             if step % 2 == 0 and step // 2 + 2 < NG:

@@ -20,8 +20,8 @@ P = 128
 PACK = 4
 CH = 128
 NCH = J // CH
-GW = 256
-NG = J // GW
+GROUPS = [(0,), (1, 2), (3, 4), (5, 6), (7,)]
+ON_VECTOR = GROUPS[3:]
 
 
 def tile_list_htabg_gate_noneP_kernel(
@@ -39,10 +39,9 @@ def tile_list_htabg_gate_noneP_kernel(
         wsc = keep.tile([P, 2, R], U8, name="wsc", align_bytes=64)
         tabw = keep.tile([P, T], I32, name="tabw", align_bytes=64)
         wb_raw = keep.tile([P, 2, R // 2], I32, name="wb_raw", align_bytes=64)
-        wd_raw = keep.tile([P, N], I32, name="wd_raw", align_bytes=64)
         wgt = keep.tile([P, J], F32, name="wgt", align_bytes=64)
         wa_raw = keep.tile([P, PACK, R], F32, name="wa_raw", align_bytes=64)
-        xp = [keep.tile([P, T], F32, name="xp%d" % i, align_bytes=64) for i in range(PACK)]
+        xp = [keep.tile([P, T], F32, name="xp0", align_bytes=64)]
         tsc0 = keep.tile([P, J], U8, name="tsc0", align_bytes=64)
         tsc1 = keep.tile([P, J], U8, name="tsc1", align_bytes=64)
         dsc = keep.tile([P, N], U8, name="dsc", align_bytes=64)
@@ -50,55 +49,67 @@ def tile_list_htabg_gate_noneP_kernel(
         nc.gpsimd.memset(wsc[:].bitcast(I32), 0)
         for q in range(4):
             nc.vector.memset(tsc[32 * q : 32 * q + 24, :].bitcast(I32), 0)
-        nc.gpsimd.memset(tsc0[:].bitcast(I32), 0)
-        nc.gpsimd.memset(tsc1[:].bitcast(I32), 0)
-        nc.gpsimd.memset(dsc[:].bitcast(I32), 0)
+        nc.vector.memset(tsc0[:].bitcast(I32), 0)
+        nc.vector.memset(tsc1[:].bitcast(I32), 0)
+        nc.vector.memset(dsc[:].bitcast(I32), 0)
         nc.sync.dma_start(idx[:], offs)
         for q in range(4):
             nc.sync.dma_start(tsc[32 * q + 24 : 32 * q + 32, :].bitcast(I32), tab_scales[:, 4 * q : 4 * q + 4, :].bitcast(I32))
-        nc.sync.dma_start(wb_raw[:], wb_words.rearrange("a p n -> p a n").bitcast(I32))
         nc.sync.dma_start(tabw[:], tab_words[0].rearrange("p t b -> p (t b)").bitcast(I32))
+        nc.sync.dma_start(wb_raw[:], wb_words.rearrange("a p n -> p a n").bitcast(I32))
         nc.sync.dma_start(idx2[:], offs2)
         for q in range(4):
-            nc.sync.dma_start(
+            nc.gpsimd.dma_start(
                 wsc[32 * q : 32 * q + 4, :, :].bitcast(I32),
                 wb_scales[:, 4 * q : 4 * q + 4, :].rearrange("a r n -> r a n").bitcast(I32),
             )
         x_planes = xT.rearrange("(p i) t -> i p t", i=PACK)
+        nc.sync.dma_start(wa_raw[:], wa.rearrange("(p i) r -> p i r", i=PACK))
         nc.sync.dma_start(wgt[:], wgt2)
         nc.sync.dma_start(xp[0][:], x_planes[0])
-        nc.sync.dma_start(xp[1][:], x_planes[1])
-        nc.sync.dma_start(xp[2][:], x_planes[2])
-        nc.sync.dma_start(wa_raw[:], wa.rearrange("(p i) r -> p i r", i=PACK))
-        nc.sync.dma_start(xp[3][:], x_planes[3])
-        nc.sync.dma_start(wd_raw[:], wd_words[0].rearrange("p n b -> p (n b)").bitcast(I32))
+
+        def load_plane(i, tag):
+            xp.append(keep.tile([P, T], F32, name="xp%d" % i, tag=tag, align_bytes=64))
+            nc.sync.dma_start(xp[i][:], x_planes[i])
 
         for q in range(4):
-            nc.sync.dma_start(dsc[32 * q : 32 * q + 4, :].bitcast(I32), wd_scales[0, 4 * q : 4 * q + 4, :].bitcast(I32))
+            nc.gpsimd.dma_start(dsc[32 * q : 32 * q + 4, :].bitcast(I32), wd_scales[0, 4 * q : 4 * q + 4, :].bitcast(I32))
         tscg = keep.tile([P, J], U8, name="tscg", align_bytes=64)
         nc.vector.tensor_copy(tscg[:], tsc[:].indirect(idx[:]))
         nc.scalar.dma_start(tsc0[0 : P - 28, :].bitcast(I32), tscg[24 : P - 4, :].bitcast(I32))
         nc.scalar.dma_start(tsc1[0 : P - 28, :].bitcast(I32), tscg[28:P, :].bitcast(I32))
+        load_plane(1, "tsc")
+        gw = keep.tile([P, J], U32, name="gw", align_bytes=64)
+        nc.vector.tensor_copy(gw[:], tabw[:].bitcast(U32).indirect(idx[:]))
+        load_plane(2, "tabw")
+        tw = keep.tile([P, 2, 2 * J], U8, name="tw", align_bytes=64)
+        nc.vector.tensor_copy(tw[:].bitcast(U16), gw[:].bitcast(U16).rearrange("p (j d) -> p d j", d=2))
+
         wbp = keep.tile([P, 2, 2 * R], U8, name="wbp", align_bytes=64)
         nc.vector.tensor_copy(
             wbp[:].bitcast(U16).rearrange("p a (t c i) -> p a c t i", t=PACK, i=8),
             wb_raw[:].bitcast(U16).rearrange("p a (c i t) -> p a c t i", t=PACK, i=8),
         )
-        gw = keep.tile([P, J], U32, name="gw", align_bytes=64)
-        nc.vector.tensor_copy(gw[:], tabw[:].bitcast(U32).indirect(idx[:]))
-        tw = keep.tile([P, 2, 2 * J], U8, name="tw", align_bytes=64)
-        nc.vector.tensor_copy(tw[:].bitcast(U16), gw[:].bitcast(U16).rearrange("p (j d) -> p d j", d=2))
-
-        wscp = keep.tile([P, 2, R], U8, name="wscp", align_bytes=64)
+        load_plane(3, "wb_raw")
+        wscp = keep.tile([P, 2, R], U8, name="wscp", tag="gw", align_bytes=64)
         nc.vector.tensor_copy(
             wscp[:].rearrange("p a (t c i) -> p a c t i", t=PACK, i=16),
             wsc[:].rearrange("p a (c i t) -> p a c t i", t=PACK, i=16),
         )
 
+        wd_raw = keep.tile([P, N], I32, name="wd_raw", tag="wsc", align_bytes=64)
+        nc.sync.dma_start(wd_raw[:], wd_words[0].rearrange("p n b -> p (n b)").bitcast(I32))
+        wa_bf = keep.tile([P, R * PACK], BF16, name="wa_bf", align_bytes=64)
+        nc.scalar.copy(
+            wa_bf[:].rearrange("p (t m i) -> p m i t", t=PACK, i=PACK), wa_raw[:].rearrange("p i (m t) -> p m i t", t=PACK)
+        )
+        wa_q = keep.tile([P, R], U32, name="wa_q", align_bytes=64)
+        wa_s = keep.tile([P, R], U8, name="wa_s", align_bytes=64)
+        nc.vector.quantize_mx(out=wa_q[:].bitcast(FP8X4), scales=wa_s[:], in_=wa_bf[:])
         tscs = (tsc0, tsc1)
         sig = []
         for c in range(NCH):
-            yb = psum.tile([P, PACK, CH], F32, name="yb", tag="yb", bufs=2)
+            yb = psum.tile([P, PACK, CH], F32, name="yb", tag="y", bufs=5)
             for t in range(PACK):
                 for a in range(2):
                     nc.tensor.matmul_mx(
@@ -114,24 +125,20 @@ def tile_list_htabg_gate_noneP_kernel(
             nc.scalar.activation(s[:], yb[:].rearrange("p t n -> p n t"), SIGMOID)
             sig.append(s)
 
-        xg = [keep.tile([P, PACK, GW], F32, name="xg%d" % g, align_bytes=64) for g in range(NG)]
+        def span(grp):
+            return slice(grp[0] * CH, (grp[-1] + 1) * CH)
 
-        def gather(i, g):
+        xg = {grp: keep.tile([P, PACK, len(grp) * CH], F32, name="xg%d" % grp[0], align_bytes=64) for grp in GROUPS}
+
+        def gather(i, grp):
+            cols = span(grp)
             nc.vector.tensor_tensor(
-                xg[g][:, i, :], xp[i][:].indirect(idx2[:, g * GW // 16 : (g + 1) * GW // 16]), wgt[:, g * GW : (g + 1) * GW], MULT
+                xg[grp][:, i, :], xp[i][:].indirect(idx2[:, cols.start // 16 : cols.stop // 16]), wgt[:, cols], MULT
             )
 
         for i in range(PACK - 1):
-            for g in range(NG):
-                gather(i, g)
-
-        wa_bf = keep.tile([P, R * PACK], BF16, name="wa_bf", tag="tw", align_bytes=64)
-        nc.scalar.copy(
-            wa_bf[:].rearrange("p (t m i) -> p m i t", t=PACK, i=PACK), wa_raw[:].rearrange("p i (m t) -> p m i t", t=PACK)
-        )
-        wa_q = keep.tile([P, R], U32, name="wa_q", align_bytes=64)
-        wa_s = keep.tile([P, R], U8, name="wa_s", align_bytes=64)
-        wdp = keep.tile([P, N], I32, name="wdp", tag="xp2", align_bytes=64)
+            for grp in GROUPS:
+                gather(i, grp)
 
         x_q = keep.tile([P, J], U32, name="x_q", align_bytes=64)
         x_s = keep.tile([P, J], U8, name="x_s", align_bytes=64)
@@ -142,109 +149,90 @@ def tile_list_htabg_gate_noneP_kernel(
         out_rows = out_0.rearrange("(p t) j -> p t j", t=PACK)
         out_words = out_1[0].rearrange("p j b -> p (j b)").bitcast(I32)
 
-        x_bf = {}
-        ya = {}
         h_bf = {}
-        yp = {}
+        x_bfs = {}
         y_bf = {}
+        y_sbs = {}
 
-        def round_x(g):
-            x_bf[g] = ring.tile([P, GW * PACK], BF16, name="x_bf", align_bytes=64)
+        def picks(grp):
+            gather(PACK - 1, grp)
+            x_bf = ring.tile([P, len(grp) * CH * PACK], BF16, name="x_bf", align_bytes=64, bufs=len(GROUPS))
+            x_bfs[grp] = x_bf
             nc.scalar.copy(
-                x_bf[g][:].rearrange("p (c e i) -> p c i e", i=PACK, e=4), xg[g][:].rearrange("p i (c e) -> p c i e", e=4)
+                x_bf[:].rearrange("p (c e i) -> p c i e", i=PACK, e=4), xg[grp][:].rearrange("p i (c e) -> p c i e", e=4)
             )
 
-        def quant_x(g):
-            cols = slice(g * GW, (g + 1) * GW)
-            nc.vector.quantize_mx(out=x_q[:, cols].bitcast(FP8X4), scales=x_s[:, cols], in_=x_bf[g][:])
-
-        def mm_a(c):
-            cols = slice(c * CH, (c + 1) * CH)
-            ya[c] = psum.tile([P, PACK, CH], F32, name="ya", tag="ya", bufs=3)
-            for t in range(PACK):
-                nc.tensor.matmul_mx(
-                    out=ya[c][:, t, :],
-                    lhsT=wa_q[:, P * t : P * (t + 1)].bitcast(FP8X4),
-                    lhsT_scale=wa_s[:, P * t : P * (t + 1)],
-                    rhs=x_q[:, cols].bitcast(FP8X4),
-                    rhs_scale=x_s[:, cols],
-                    start=True,
-                    stop=True,
+        def gate(grp):
+            nc.vector.quantize_mx(out=x_q[:, span(grp)].bitcast(FP8X4), scales=x_s[:, span(grp)], in_=x_bfs[grp][:])
+            h_bf[grp] = ring.tile([P, len(grp) * CH * PACK], BF16, name="h_bf", align_bytes=64)
+            for u, c in enumerate(grp):
+                cols = slice(c * CH, (c + 1) * CH)
+                ya = psum.tile([P, PACK, CH], F32, name="ya", tag="ya", bufs=3)
+                for t in range(PACK):
+                    nc.tensor.matmul_mx(
+                        out=ya[:, t, :],
+                        lhsT=wa_q[:, P * t : P * (t + 1)].bitcast(FP8X4),
+                        lhsT_scale=wa_s[:, P * t : P * (t + 1)],
+                        rhs=x_q[:, cols].bitcast(FP8X4),
+                        rhs_scale=x_s[:, cols],
+                        start=True,
+                        stop=True,
+                    )
+                nc.vector.tensor_tensor(
+                    h_bf[grp][:, u * CH * PACK : (u + 1) * CH * PACK].rearrange("p (n t) -> p n t", t=PACK),
+                    ya[:].rearrange("p t n -> p n t"),
+                    sig[c][:],
+                    MULT,
                 )
 
-        def gate(c):
-            h_bf[c] = ring.tile([P, CH, PACK], BF16, name="h_bf", align_bytes=64)
-            nc.vector.tensor_tensor(h_bf[c][:], ya[c][:].rearrange("p t n -> p n t"), sig[c][:], MULT)
+        def second(grp, wdp):
+            nc.vector.quantize_mx(out=h_q[:, span(grp)].bitcast(FP8X4), scales=h_s[:, span(grp)], in_=h_bf[grp][:])
+            y_sb = ring.tile([P, PACK, len(grp) * CH], F32, name="y_sb", align_bytes=64, bufs=len(GROUPS))
+            y_bf[grp] = ring.tile([P, len(grp) * CH * PACK], BF16, name="y_bf", align_bytes=64, bufs=len(GROUPS))
+            for u, c in enumerate(grp):
+                cols = slice(c * CH, (c + 1) * CH)
+                yp = psum.tile([P, PACK, CH], F32, name="yp", tag="y", bufs=5)
+                for t in range(PACK):
+                    nc.tensor.matmul_mx(
+                        out=yp[:, t, :],
+                        lhsT=wdp[:, P * t : P * (t + 1)].bitcast(FP8X4),
+                        lhsT_scale=dscp[:, P * t : P * (t + 1)],
+                        rhs=h_q[:, cols].bitcast(FP8X4),
+                        rhs_scale=h_s[:, cols],
+                        start=True,
+                        stop=True,
+                    )
+                rounded = y_bf[grp][:, u * CH * PACK : (u + 1) * CH * PACK]
+                nc.scalar.copy(y_sb[:, :, u * CH : (u + 1) * CH], yp[:])
+                if grp not in ON_VECTOR:
+                    nc.scalar.copy(rounded.rearrange("p (n t) -> p n t", t=PACK), yp[:].rearrange("p t n -> p n t"))
+            y_sbs[grp] = y_sb
+            nc.sync.dma_start(out_rows[:, :, span(grp)], y_sb[:])
 
-        def quant_h(c):
-            cols = slice(c * CH, (c + 1) * CH)
-            nc.vector.quantize_mx(
-                out=h_q[:, cols].bitcast(FP8X4), scales=h_s[:, cols], in_=h_bf[c][:].rearrange("p n t -> p (n t)")
-            )
-
-        def mm_d(c):
-            cols = slice(c * CH, (c + 1) * CH)
-            yp[c] = psum.tile([P, PACK, CH], F32, name="yp", tag="yp", bufs=3)
-            for t in range(PACK):
-                nc.tensor.matmul_mx(
-                    out=yp[c][:, t, :],
-                    lhsT=wdp[:, P * t : P * (t + 1)].bitcast(FP8X4),
-                    lhsT_scale=dscp[:, P * t : P * (t + 1)],
-                    rhs=h_q[:, cols].bitcast(FP8X4),
-                    rhs_scale=h_s[:, cols],
-                    start=True,
-                    stop=True,
-                )
-
-        def out_y(c):
-            cols = slice(c * CH, (c + 1) * CH)
-            y_sb = ring.tile([P, PACK, CH], F32, name="y_sb", align_bytes=64, bufs=4)
-            y_bf[c] = ring.tile([P, CH * PACK], BF16, name="y_bf", align_bytes=64)
-            nc.scalar.copy(y_sb[:], yp[c][:])
-            if c % 2 == 0:
-                nc.scalar.copy(y_bf[c][:].rearrange("p (n t) -> p n t", t=PACK), yp[c][:].rearrange("p t n -> p n t"))
-            else:
+        def planes(grp):
+            if grp in ON_VECTOR:
                 nc.vector.tensor_copy(
-                    y_bf[c][:].rearrange("p (c e t) -> p c t e", t=PACK, e=4), y_sb[:].rearrange("p t (c e) -> p c t e", e=4)
+                    y_bf[grp][:].rearrange("p (c e t) -> p c t e", t=PACK, e=4),
+                    y_sbs[grp][:].rearrange("p t (c e) -> p c t e", e=4),
                 )
-            nc.sync.dma_start(out_rows[:, :, cols], y_sb[:])
+            nc.vector.quantize_mx(out=y_q[:, span(grp)].bitcast(FP8X4), scales=y_s[:, span(grp)], in_=y_bf[grp][:])
+            nc.sync.dma_start(out_words[:, span(grp)], y_q[:, span(grp)].bitcast(I32))
 
-        def quant_y(c):
-            cols = slice(c * CH, (c + 1) * CH)
-            nc.vector.quantize_mx(out=y_q[:, cols].bitcast(FP8X4), scales=y_s[:, cols], in_=y_bf[c][:])
-            if c % 2 == 1:
-                pair = slice((c - 1) * CH, (c + 1) * CH)
-                nc.sync.dma_start(out_words[:, pair], y_q[:, pair].bitcast(I32))
-
-        gather(PACK - 1, 0)
-        round_x(0)
-        nc.vector.quantize_mx(out=wa_q[:].bitcast(FP8X4), scales=wa_s[:], in_=wa_bf[:])
-        gather(PACK - 1, 1)
-        round_x(1)
-        quant_x(0)
-        nc.vector.tensor_copy(
-            wdp[:].rearrange("p (t c i) -> p c t i", t=PACK, i=4), wd_raw[:].rearrange("p (c i t) -> p c t i", t=PACK, i=4)
-        )
-        dscp = keep.tile([P, N], U8, name="dscp", tag="wa_raw", align_bytes=64)
+        dscp = keep.tile([P, N], U8, name="dscp", tag="tabw", align_bytes=64)
         nc.vector.tensor_copy(
             dscp[:].rearrange("p (t c i) -> p c t i", t=PACK, i=16), dsc[:].rearrange("p (c i t) -> p c t i", t=PACK, i=16)
         )
-        for step in range(NCH + 3):
-            if step % 2 == 0 and step // 2 + 2 < NG:
-                gather(PACK - 1, step // 2 + 2)
-                round_x(step // 2 + 2)
-            if step % 2 == 1 and (step + 1) // 2 < NG:
-                quant_x((step + 1) // 2)
-            if step < NCH:
-                mm_a(step)
-                gate(step)
-            if 0 <= step - 1 < NCH:
-                quant_h(step - 1)
-                mm_d(step - 1)
-            if 0 <= step - 2 < NCH:
-                out_y(step - 2)
-            if 0 <= step - 3 < NCH:
-                quant_y(step - 3)
+        for grp in GROUPS:
+            picks(grp)
+        wdp = keep.tile([P, N], I32, name="wdp", tag="wb_raw", align_bytes=64)
+        nc.vector.tensor_copy(
+            wdp[:].rearrange("p (t c i) -> p c t i", t=PACK, i=4), wd_raw[:].rearrange("p (c i t) -> p c t i", t=PACK, i=4)
+        )
+        for grp in GROUPS:
+            gate(grp)
+            second(grp, wdp)
+        for grp in GROUPS:
+            planes(grp)
         for q in range(4):
             eng = nc.scalar if q % 2 else nc.sync
             eng.dma_start(out_2[0, 4 * q : 4 * q + 4, :].bitcast(I32), y_s[32 * q : 32 * q + 4, :].bitcast(I32))

from contextlib import ExitStack

import concourse.mybir as mybir

K, L, R, N, T, J = 512, 1024, 512, 512, 2048, 1024
FLOPS = 2 * J * (K * R + L * R + R * N)

F32 = mybir.dt.float32
BF16 = mybir.dt.bfloat16
I32 = mybir.dt.int32
U32 = mybir.dt.uint32
U16 = mybir.dt.uint16
U8 = mybir.dt.uint8
FP8X4 = mybir.dt.float8_e4m3fn_x4
FP4X4 = mybir.dt.float4_e2m1fn_x4
MULT = mybir.AluOpType.mult
SIGMOID = mybir.ActivationFunctionType.Sigmoid

P = 128
PACK = 4
CH = 128
NCH = J // CH
GROUPS = [(0,), (1, 2), (3, 4), (5, 6), (7,)]
ON_VECTOR = GROUPS[3:]


def tile_list_htabg_gate_noneP_kernel(
    tc, tab_words, tab_scales, xT, wgt2, wa, wb_words, wb_scales, wd_words, wd_scales, offs, offs2, out_0, out_1, out_2
):
    nc = tc.nc
    with ExitStack() as ctx:
        keep = ctx.enter_context(tc.tile_pool(name="keep", bufs=1))
        ring = ctx.enter_context(tc.tile_pool(name="ring", bufs=3))
        psum = ctx.enter_context(tc.psum_pool(name="psum", bufs=1))

        idx = keep.tile([P, J // 16], U16, name="idx")
        idx2 = keep.tile([P, J // 16], U16, name="idx2")
        tsc = keep.tile([P, T], U8, name="tsc", align_bytes=64)
        wsc = keep.tile([P, 2, R], U8, name="wsc", align_bytes=64)
        tabw = keep.tile([P, T], I32, name="tabw", align_bytes=64)
        wb_raw = keep.tile([P, 2, R // 2], I32, name="wb_raw", align_bytes=64)
        wgt = keep.tile([P, J], F32, name="wgt", align_bytes=64)
        wa_raw = keep.tile([P, PACK, R], F32, name="wa_raw", align_bytes=64)
        xp = [keep.tile([P, T], F32, name="xp0", align_bytes=64)]
        tsc0 = keep.tile([P, J], U8, name="tsc0", align_bytes=64)
        tsc1 = keep.tile([P, J], U8, name="tsc1", align_bytes=64)
        dsc = keep.tile([P, N], U8, name="dsc", align_bytes=64)

        nc.gpsimd.memset(wsc[:].bitcast(I32), 0)
        for q in range(4):
            nc.vector.memset(tsc[32 * q : 32 * q + 24, :].bitcast(I32), 0)
        nc.vector.memset(tsc0[:].bitcast(I32), 0)
        nc.vector.memset(tsc1[:].bitcast(I32), 0)
        nc.vector.memset(dsc[:].bitcast(I32), 0)
        nc.sync.dma_start(idx[:], offs)
        for q in range(4):
            nc.sync.dma_start(tsc[32 * q + 24 : 32 * q + 32, :].bitcast(I32), tab_scales[:, 4 * q : 4 * q + 4, :].bitcast(I32))
        nc.sync.dma_start(tabw[:], tab_words[0].rearrange("p t b -> p (t b)").bitcast(I32))
        nc.sync.dma_start(wb_raw[:], wb_words.rearrange("a p n -> p a n").bitcast(I32))
        nc.sync.dma_start(idx2[:], offs2)
        for q in range(4):
            nc.gpsimd.dma_start(
                wsc[32 * q : 32 * q + 4, :, :].bitcast(I32),
                wb_scales[:, 4 * q : 4 * q + 4, :].rearrange("a r n -> r a n").bitcast(I32),
            )
        x_planes = xT.rearrange("(p i) t -> i p t", i=PACK)
        nc.sync.dma_start(wa_raw[:], wa.rearrange("(p i) r -> p i r", i=PACK))
        nc.sync.dma_start(wgt[:], wgt2)
        nc.sync.dma_start(xp[0][:], x_planes[0])

        def load_plane(i, tag):
            xp.append(keep.tile([P, T], F32, name="xp%d" % i, tag=tag, align_bytes=64))
            nc.sync.dma_start(xp[i][:], x_planes[i])

        for q in range(4):
            nc.gpsimd.dma_start(dsc[32 * q : 32 * q + 4, :].bitcast(I32), wd_scales[0, 4 * q : 4 * q + 4, :].bitcast(I32))
        tscg = keep.tile([P, J], U8, name="tscg", align_bytes=64)
        nc.vector.tensor_copy(tscg[:], tsc[:].indirect(idx[:]))
        nc.scalar.dma_start(tsc0[0 : P - 28, :].bitcast(I32), tscg[24 : P - 4, :].bitcast(I32))
        nc.scalar.dma_start(tsc1[0 : P - 28, :].bitcast(I32), tscg[28:P, :].bitcast(I32))
        load_plane(1, "tsc")
        gw = keep.tile([P, J], U32, name="gw", align_bytes=64)
        nc.vector.tensor_copy(gw[:], tabw[:].bitcast(U32).indirect(idx[:]))
        load_plane(2, "tabw")
        tw = keep.tile([P, 2, 2 * J], U8, name="tw", align_bytes=64)
        nc.vector.tensor_copy(tw[:].bitcast(U16), gw[:].bitcast(U16).rearrange("p (j d) -> p d j", d=2))

        wbp = keep.tile([P, 2, 2 * R], U8, name="wbp", align_bytes=64)
        nc.vector.tensor_copy(
            wbp[:].bitcast(U16).rearrange("p a (t c i) -> p a c t i", t=PACK, i=8),
            wb_raw[:].bitcast(U16).rearrange("p a (c i t) -> p a c t i", t=PACK, i=8),
        )
        load_plane(3, "wb_raw")
        wscp = keep.tile([P, 2, R], U8, name="wscp", tag="gw", align_bytes=64)
        nc.vector.tensor_copy(
            wscp[:].rearrange("p a (t c i) -> p a c t i", t=PACK, i=16),
            wsc[:].rearrange("p a (c i t) -> p a c t i", t=PACK, i=16),
        )

        wd_raw = keep.tile([P, N], I32, name="wd_raw", tag="wsc", align_bytes=64)
        nc.sync.dma_start(wd_raw[:], wd_words[0].rearrange("p n b -> p (n b)").bitcast(I32))
        wa_bf = keep.tile([P, R * PACK], BF16, name="wa_bf", align_bytes=64)
        nc.scalar.copy(
            wa_bf[:].rearrange("p (t m i) -> p m i t", t=PACK, i=PACK), wa_raw[:].rearrange("p i (m t) -> p m i t", t=PACK)
        )
        wa_q = keep.tile([P, R], U32, name="wa_q", align_bytes=64)
        wa_s = keep.tile([P, R], U8, name="wa_s", align_bytes=64)
        nc.vector.quantize_mx(out=wa_q[:].bitcast(FP8X4), scales=wa_s[:], in_=wa_bf[:])
        tscs = (tsc0, tsc1)
        sig = []
        for c in range(NCH):
            yb = psum.tile([P, PACK, CH], F32, name="yb", tag="y", bufs=5)
            for t in range(PACK):
                for a in range(2):
                    nc.tensor.matmul_mx(
                        out=yb[:, t, :],
                        lhsT=wbp[:, a, 2 * P * t : 2 * P * (t + 1)].bitcast(FP4X4),
                        lhsT_scale=wscp[:, a, P * t : P * (t + 1)],
                        rhs=tw[:, a, 2 * CH * c : 2 * CH * (c + 1)].bitcast(FP4X4),
                        rhs_scale=tscs[a][:, CH * c : CH * (c + 1)],
                        start=(a == 0),
                        stop=(a == 1),
                    )
            s = keep.tile([P, CH, PACK], F32, name="sig%d" % c, align_bytes=64)
            nc.scalar.activation(s[:], yb[:].rearrange("p t n -> p n t"), SIGMOID)
            sig.append(s)

        def span(grp):
            return slice(grp[0] * CH, (grp[-1] + 1) * CH)

        xg = {grp: keep.tile([P, PACK, len(grp) * CH], F32, name="xg%d" % grp[0], align_bytes=64) for grp in GROUPS}

        def gather(i, grp):
            cols = span(grp)
            nc.vector.tensor_tensor(
                xg[grp][:, i, :], xp[i][:].indirect(idx2[:, cols.start // 16 : cols.stop // 16]), wgt[:, cols], MULT
            )

        for i in range(PACK - 1):
            for grp in GROUPS:
                gather(i, grp)

        x_q = keep.tile([P, J], U32, name="x_q", align_bytes=64)
        x_s = keep.tile([P, J], U8, name="x_s", align_bytes=64)
        h_q = keep.tile([P, J], U32, name="h_q", align_bytes=64)
        h_s = keep.tile([P, J], U8, name="h_s", align_bytes=64)
        y_q = keep.tile([P, J], U32, name="y_q", align_bytes=64)
        y_s = keep.tile([P, J], U8, name="y_s", align_bytes=64)
        out_rows = out_0.rearrange("(p t) j -> p t j", t=PACK)
        out_words = out_1[0].rearrange("p j b -> p (j b)").bitcast(I32)

        h_bf = {}
        x_bfs = {}
        y_bf = {}
        y_sbs = {}

        def picks(grp):
            gather(PACK - 1, grp)
            x_bf = ring.tile([P, len(grp) * CH * PACK], BF16, name="x_bf", align_bytes=64, bufs=len(GROUPS))
            x_bfs[grp] = x_bf
            nc.scalar.copy(
                x_bf[:].rearrange("p (c e i) -> p c i e", i=PACK, e=4), xg[grp][:].rearrange("p i (c e) -> p c i e", e=4)
            )

        def gate(grp):
            nc.vector.quantize_mx(out=x_q[:, span(grp)].bitcast(FP8X4), scales=x_s[:, span(grp)], in_=x_bfs[grp][:])
            h_bf[grp] = ring.tile([P, len(grp) * CH * PACK], BF16, name="h_bf", align_bytes=64)
            for u, c in enumerate(grp):
                cols = slice(c * CH, (c + 1) * CH)
                ya = psum.tile([P, PACK, CH], F32, name="ya", tag="ya", bufs=3)
                for t in range(PACK):
                    nc.tensor.matmul_mx(
                        out=ya[:, t, :],
                        lhsT=wa_q[:, P * t : P * (t + 1)].bitcast(FP8X4),
                        lhsT_scale=wa_s[:, P * t : P * (t + 1)],
                        rhs=x_q[:, cols].bitcast(FP8X4),
                        rhs_scale=x_s[:, cols],
                        start=True,
                        stop=True,
                    )
                nc.vector.tensor_tensor(
                    h_bf[grp][:, u * CH * PACK : (u + 1) * CH * PACK].rearrange("p (n t) -> p n t", t=PACK),
                    ya[:].rearrange("p t n -> p n t"),
                    sig[c][:],
                    MULT,
                )

        def second(grp, wdp):
            nc.vector.quantize_mx(out=h_q[:, span(grp)].bitcast(FP8X4), scales=h_s[:, span(grp)], in_=h_bf[grp][:])
            y_sb = ring.tile([P, PACK, len(grp) * CH], F32, name="y_sb", align_bytes=64, bufs=len(GROUPS))
            y_bf[grp] = ring.tile([P, len(grp) * CH * PACK], BF16, name="y_bf", align_bytes=64, bufs=len(GROUPS))
            for u, c in enumerate(grp):
                cols = slice(c * CH, (c + 1) * CH)
                yp = psum.tile([P, PACK, CH], F32, name="yp", tag="y", bufs=5)
                for t in range(PACK):
                    nc.tensor.matmul_mx(
                        out=yp[:, t, :],
                        lhsT=wdp[:, P * t : P * (t + 1)].bitcast(FP8X4),
                        lhsT_scale=dscp[:, P * t : P * (t + 1)],
                        rhs=h_q[:, cols].bitcast(FP8X4),
                        rhs_scale=h_s[:, cols],
                        start=True,
                        stop=True,
                    )
                rounded = y_bf[grp][:, u * CH * PACK : (u + 1) * CH * PACK]
                nc.scalar.copy(y_sb[:, :, u * CH : (u + 1) * CH], yp[:])
                if grp not in ON_VECTOR:
                    nc.scalar.copy(rounded.rearrange("p (n t) -> p n t", t=PACK), yp[:].rearrange("p t n -> p n t"))
            y_sbs[grp] = y_sb
            nc.sync.dma_start(out_rows[:, :, span(grp)], y_sb[:])

        def planes(grp):
            if grp in ON_VECTOR:
                nc.vector.tensor_copy(
                    y_bf[grp][:].rearrange("p (c e t) -> p c t e", t=PACK, e=4),
                    y_sbs[grp][:].rearrange("p t (c e) -> p c t e", e=4),
                )
            nc.vector.quantize_mx(out=y_q[:, span(grp)].bitcast(FP8X4), scales=y_s[:, span(grp)], in_=y_bf[grp][:])
            nc.sync.dma_start(out_words[:, span(grp)], y_q[:, span(grp)].bitcast(I32))

        dscp = keep.tile([P, N], U8, name="dscp", tag="tabw", align_bytes=64)
        nc.vector.tensor_copy(
            dscp[:].rearrange("p (t c i) -> p c t i", t=PACK, i=16), dsc[:].rearrange("p (c i t) -> p c t i", t=PACK, i=16)
        )
        for grp in GROUPS:
            picks(grp)
        wdp = keep.tile([P, N], I32, name="wdp", tag="wb_raw", align_bytes=64)
        nc.vector.tensor_copy(
            wdp[:].rearrange("p (t c i) -> p c t i", t=PACK, i=4), wd_raw[:].rearrange("p (c i t) -> p c t i", t=PACK, i=4)
        )
        for grp in GROUPS:
            gate(grp)
            second(grp, wdp)
        for grp in GROUPS:
            planes(grp)
        for q in range(4):
            eng = nc.scalar if q % 2 else nc.sync
            eng.dma_start(out_2[0, 4 * q : 4 * q + 4, :].bitcast(I32), y_s[32 * q : 32 * q + 4, :].bitcast(I32))
